import numpy as np
import ml_dtypes


def mxq(x, axis, fmt="e4m3"):
    dtype, down = {"e4m3": (ml_dtypes.float8_e4m3fn, 7), "e5m2": (ml_dtypes.float8_e5m2, 14)}[fmt]
    v = np.moveaxis(np.asarray(x, np.float32).astype(ml_dtypes.bfloat16).astype(np.float64), axis, -1)
    blocks = v.reshape(v.shape[:-1] + (-1, 32))
    amax = np.abs(blocks).max(-1, keepdims=True)
    byte = np.maximum(np.where(amax > 0, np.frexp(amax)[1] - 1 + 127, 0) - down, 1)
    scale = np.exp2(byte - 127.0)
    codes = (blocks / scale).astype(np.float32).astype(dtype).astype(np.float64)
    return np.moveaxis((codes * scale).reshape(v.shape), -1, axis)


WIDE = False


def mx_kscale(k):
    if not WIDE:
        return np.ones(k)
    levels = np.array([10, -10, 5, -5, 0])
    if k % 512:
        return np.exp2(np.random.permutation(np.resize(levels, k // 32))).repeat(32)
    a = np.empty((k // 512, 16))
    for p in range(k // 512):
        a[p, :8] = np.random.permutation(np.resize(levels, 8))
        for g in range(8):
            far = levels[np.abs(levels - a[p, g]) >= 10]
            a[p, g + 8] = far[np.random.randint(len(far))]
    return np.exp2(a.ravel()).repeat(32)


def f64(x):
    return np.asarray(x).astype(np.float64)


def striped(idx):
    return np.tile(idx.reshape(-1, 16).T, (8, 1)).astype(np.uint16)


def unstriped(offs):
    return offs[:16].T.reshape(-1).astype(np.int64)


def striped8(idx):
    return np.concatenate([x.reshape(-1, 16).T for x in idx]).astype(np.uint16)


def runs(offs, k):
    lists = np.stack([offs[16 * r : 16 * r + 16].T.reshape(-1) for r in range(8)]).astype(np.int64)
    return lists[np.arange(k) % 512 // 64]


def pack_weight(w):
    k, n = w.shape
    w = f64(np.asarray(w, np.float32).astype(ml_dtypes.bfloat16)).reshape(k // 32, 32, n)
    amax = np.abs(w).max(1)
    byte = np.clip(np.where(amax > 0, np.frexp(amax)[1] - 1 + 127 - 7, 1), 1, 254)
    scaled = (w * np.exp2(127.0 - byte)[:, None, :]).reshape(k, n).astype(np.float32)
    words = np.ascontiguousarray(scaled.reshape(k // 512, 128, 4, n).transpose(0, 1, 3, 2)).astype(ml_dtypes.float8_e4m3fn).view(np.uint8)
    return words, np.ascontiguousarray(byte.astype(np.uint8).reshape(k // 512, 16, n))


def unpack_weight(words, scales):
    g, p, n, _ = words.shape
    vals = np.ascontiguousarray(words).view(ml_dtypes.float8_e4m3fn).astype(np.float64) * np.repeat(np.exp2(scales.astype(np.float64) - 127.0), 8, axis=1)[..., None]
    return vals.transpose(0, 1, 3, 2).reshape(g * 512, n)


def sigmoid(v):
    return 1.0 / (1.0 + np.exp(-np.maximum(v, -700.0)))

def planes(y):
    n, m = y.shape
    v = y.astype(np.float32).astype(ml_dtypes.bfloat16).astype(np.float64).reshape(n // 32, 32, m)
    top = np.abs(v).max(1)
    byte = np.clip(np.where(top > 0, np.frexp(top)[1] - 1 + 127 - 7, 1), 1, 254)
    codes = (v * np.exp2(127.0 - byte)[:, None, :]).reshape(n, m).astype(np.float32).astype(ml_dtypes.float8_e4m3fn).view(np.uint8)
    words = codes.reshape(n // 512, 128, 4, m).transpose(0, 1, 3, 2)
    return np.ascontiguousarray(words), np.ascontiguousarray(byte.astype(np.uint8).reshape(n // 512, 16, m))


K, T, S, N, H = 512, 2048, 512, 512, 512


def setup_inputs():
    n = np.random.standard_normal
    s = mx_kscale(K)[:, None]
    u = mx_kscale(S)
    packed_xT = pack_weight(n((K, T)) * s)
    return {
        "x_words": packed_xT[0],
        "x_scales": packed_xT[1],
        "wa": (n((K, H)) / np.sqrt(K) / s).astype(np.float32),
        "wb": (n((K, N)) / np.sqrt(K) / s).astype(np.float32),
        "gt": (np.random.uniform(0.5, 1.5, (S, 1)) * u[:, None]).astype(np.float32),
        "gi": (np.random.uniform(0.5, 1.5, (S, 1)) / u[:, None]).astype(np.float32),
        "offs": striped(np.random.permutation(T)[:S]),
        "two": striped(np.random.permutation(T)[:S]),
        "n1": striped8(np.stack([np.random.permutation(H) for _ in range(8)])),
        "n2": striped8(np.stack([np.random.permutation(H) for _ in range(8)])),
        "n3": striped8(np.stack([np.random.permutation(N) for _ in range(8)])),
        "n4": striped8(np.stack([np.random.permutation(N) for _ in range(8)])),
        "n5": striped8(np.stack([np.random.permutation(N) for _ in range(8)])),
        "n6": striped8(np.stack([np.random.permutation(N) for _ in range(8)])),
        "n7": striped8(np.stack([np.random.permutation(N) for _ in range(8)])),
    }


def reference(x_words, x_scales, wa, wb, gt, gi, offs, two, n1, n2, n3, n4, n5, n6, n7):
    xq = unpack_weight(x_words, x_scales)[:, unstriped(offs)]
    a = xq.T @ mxq(f64(wa), 0, "e4m3")
    z = f64(gt) * (np.maximum(a * (sigmoid(a[np.arange(S)[:, None], runs(n1, S)])), a[np.arange(S)[:, None], runs(n2, S)]))
    x_two = unpack_weight(x_words, x_scales)[:, unstriped(two)]
    b = x_two.T @ mxq(f64(wb), 0, "e4m3")
    z2 = f64(gi) * (np.minimum(np.maximum(b, b[np.arange(S)[:, None], runs(n3, S)]), b[np.arange(S)[:, None], runs(n4, S)]))
    cv = 0.0625 * ((mxq(z, 0, "e4m3").T @ mxq(z2, 0, "e4m3")))
    out_0 = (cv[np.arange(H)[:, None], runs(n5, H)]) * sigmoid(cv) + (cv[np.arange(H)[:, None], runs(n6, H)]) * (sigmoid(cv[np.arange(H)[:, None], runs(n7, H)]))
    return (out_0,) + planes(out_0)

@@ -1,0 +1,285 @@
+from contextlib import ExitStack
+
+import concourse.mybir as mybir
+
+K, T, S, N, H = 512, 2048, 512, 512, 512
+FLOPS = 2 * K * S * H + 2 * K * S * N + 2 * S * H * N
+
+F32 = mybir.dt.float32
+BF16 = mybir.dt.bfloat16
+I32 = mybir.dt.int32
+U32 = mybir.dt.uint32
+U16 = mybir.dt.uint16
+U8 = mybir.dt.uint8
+FP8X4 = mybir.dt.float8_e4m3fn_x4
+ALU = mybir.AluOpType
+ACT = mybir.ActivationFunctionType
+
+P = 128
+PACK = 4
+W = 512
+HALF = 256
+LCOLS = HALF // 16
+
+
+def tile_picked_mombgmaxminmxwsum_none_po_kernel(tc, x_words, x_scales, wa, wb, gt, gi, offs, two, n1, n2, n3, n4, n5, n6, n7, out_0, out_1, out_2):
+    nc = tc.nc
+    with ExitStack() as ctx:
+        sb = ctx.enter_context(tc.tile_pool(name="sb", bufs=1))
+        ps = ctx.enter_context(tc.psum_pool(name="ps", bufs=1))
+
+        def tile(name, shape, dtype):
+            return sb.tile(shape, dtype, name=name, align_bytes=64)
+
+        def tiles(name, shape, dtype, count=PACK):
+            return [tile("%s%d" % (name, i), shape, dtype) for i in range(count)]
+
+        def cols(h):
+            return slice(h * HALF, (h + 1) * HALF)
+
+        def look(window, lst, h):
+            return window[:].indirect(lst[:, h * LCOLS : (h + 1) * LCOLS])
+
+        lists = {}
+        for name in ("two", "offs", "n1", "n2", "n3", "n4", "n5", "n6", "n7"):
+            lists[name] = tile("list_" + name, [P, S // 16], U16)
+
+        xs = tile("xs", [P, T], U8)
+        xw = tile("xw", [P, T], U32)
+        wb_raw = tiles("wb_raw", [P, PACK, HALF], F32, 2)
+        wa_raw = tiles("wa_raw", [P, PACK, HALF], F32, 2)
+        gt_sb = tile("gt_sb", [P, PACK], F32)
+        gi_sb = tile("gi_sb", [P, PACK], F32)
+
+        warm = tile("warm", [P, 2], F32)
+        nc.vector.memset(xs[:].bitcast(I32), 0)
+        nc.gpsimd.memset(warm[:, 0:1], 0.0)
+        nc.scalar.activation(warm[:, 1:2], warm[:, 0:1], ACT.Sigmoid)
+
+        nc.sync.dma_start(lists["two"][:], two)
+        scale_rows = x_scales[0].bitcast(I32)
+        for q in range(4):
+            nc.sync.dma_start(xs[32 * q : 32 * q + 4, :].bitcast(I32), scale_rows[4 * q : 4 * q + 4, :])
+        nc.sync.dma_start(lists["offs"][:], offs)
+        wb_rows = wb.rearrange("(p j) c -> p j c", j=PACK)
+        wa_rows = wa.rearrange("(p j) c -> p j c", j=PACK)
+        for h in range(2):
+            nc.sync.dma_start(wb_raw[h][:], wb_rows[:, :, cols(h)])
+        nc.sync.dma_start(xw[:].bitcast(I32), x_words[0].rearrange("p n r -> p (n r)").bitcast(I32))
+        nc.sync.dma_start(gi_sb[:], gi.rearrange("(p t) o -> p (t o)", t=PACK))
+        nc.sync.dma_start(gt_sb[:], gt.rearrange("(p t) o -> p (t o)", t=PACK))
+        nc.sync.dma_start(lists["n3"][:], n3)
+        nc.sync.dma_start(lists["n4"][:], n4)
+        for h in range(2):
+            nc.sync.dma_start(wa_raw[h][:], wa_rows[:, :, cols(h)])
+        for name, src in (("n1", n1), ("n2", n2), ("n5", n5), ("n6", n6), ("n7", n7)):
+            nc.sync.dma_start(lists[name][:], src)
+
+        def pick_scales(name):
+            got = tile("got_" + name, [P, S], U8)
+            dealt = tile("dealt_" + name, [P, S], U8)
+            nc.vector.tensor_copy(got[:], xs[:].indirect(lists[name][:]))
+            return got, dealt
+
+        def deal_scales(got, dealt):
+            nc.vector.tensor_copy(
+                dealt[:].rearrange("p (t m) -> p t m", t=PACK), got[:].rearrange("p (m t) -> p t m", t=PACK)
+            )
+
+        def pick_words(name):
+            words = tile("words_" + name, [P, S], U32)
+            nc.vector.tensor_copy(words[:].rearrange("p (t m) -> p m t", t=PACK), xw[:].indirect(lists[name][:]))
+            return words
+
+        def weave(copy, dst, src):
+            copy(dst.rearrange("p (c i t) -> p c t i", i=4, t=PACK), src.rearrange("p t (c i) -> p c t i", i=4))
+
+        def quantize(codes, scales, src):
+            nc.vector.quantize_mx(out=codes.bitcast(FP8X4), scales=scales, in_=src)
+
+        def product(bank, l_codes, l_scales, t, r_codes, r_scales):
+            m = slice(t * P, (t + 1) * P)
+            nc.tensor.matmul_mx(
+                out=bank[:], lhsT=l_codes[:, m].bitcast(FP8X4), lhsT_scale=l_scales[:, m],
+                rhs=r_codes[:].bitcast(FP8X4), rhs_scale=r_scales[:], start=True, stop=True,
+            )
+
+        got_b, xs_b = pick_scales("two")
+        got_a, xs_a = pick_scales("offs")
+        deal_scales(got_b, xs_b)
+        deal_scales(got_a, xs_a)
+
+        wb_bf = tiles("wb_bf", [P, PACK * HALF], BF16, 2)
+        wb_codes = tile("wb_codes", [P, W], U32)
+        wb_scales = tile("wb_scales", [P, W], U8)
+        for h in range(2):
+            weave(nc.scalar.copy, wb_bf[h][:], wb_raw[h][:])
+        for h in range(2):
+            quantize(wb_codes[:, cols(h)], wb_scales[:, cols(h)], wb_bf[h][:])
+        xw_b = pick_words("two")
+
+        sign = tile("sign", [P, PACK], F32)
+        gi_abs = tile("gi_abs", [P, PACK], F32)
+        gt_signed = tile("gt_signed", [P, PACK], F32)
+        nc.vector.tensor_scalar(sign[:], gi_sb[:], 0.0, 2.0, ALU.is_ge, ALU.mult)
+        nc.vector.scalar_tensor_tensor(gi_abs[:], gi_sb[:], -1.0, gi_sb[:], ALU.mult, ALU.max)
+        nc.vector.scalar_tensor_tensor(gt_signed[:], sign[:], 1.0, gt_sb[:], ALU.subtract, ALU.mult)
+
+        b_ps = [ps.tile([P, W], F32, name="b_ps%d" % t, tag="bank%d" % t) for t in range(PACK)]
+        a_ps = [ps.tile([P, W], F32, name="a_ps%d" % t, tag="bank%d" % (PACK + t)) for t in range(PACK)]
+        for t in range(PACK):
+            product(b_ps[t], xw_b, xs_b, t, wb_codes, wb_scales)
+        xw_a = pick_words("offs")
+
+        b_win = tiles("b_win", [P, W], F32)
+        b_bf = tiles("b_bf", [P, W], BF16)
+        b3 = tiles("b3", [P, W], BF16)
+        b4 = tiles("b4", [P, W], BF16)
+        z2_rows = tile("z2_rows", [P, PACK, W], BF16)
+        wa_bf = tiles("wa_bf", [P, PACK * HALF], BF16, 2)
+        wa_codes = tile("wa_codes", [P, W], U32)
+        wa_scales = tile("wa_scales", [P, W], U8)
+        a_win = tiles("a_win", [P, W], F32)
+        s1 = tiles("s1", [P, W], F32)
+
+        def b_out(t):
+            nc.scalar.activation(b_win[t][:], b_ps[t][:], ACT.Copy, scale=gi_abs[:, t : t + 1])
+            nc.scalar.activation(b_bf[t][:], b_ps[t][:], ACT.Copy, scale=gi_abs[:, t : t + 1])
+
+        def b_fetch(t):
+            for h in range(2):
+                nc.vector.tensor_copy(b3[t][:, cols(h)], look(b_win[t], lists["n3"], h))
+            for h in range(2):
+                nc.vector.tensor_copy(b4[t][:, cols(h)], look(b_win[t], lists["n4"], h))
+
+        def b_max(t):
+            nc.vector.tensor_tensor(b3[t][:], b3[t][:], b_bf[t][:], ALU.max)
+
+        def b_min(t):
+            nc.vector.tensor_tensor(z2_rows[:, t, :], b3[t][:], b4[t][:], ALU.min)
+
+        def a_out(t):
+            nc.scalar.copy(a_win[t][:], a_ps[t][:])
+            for h in range(2):
+                nc.scalar.activation(s1[t][:, cols(h)], look(a_win[t], lists["n1"], h), ACT.Sigmoid)
+
+        b_out(0)
+        b_out(1)
+        b_fetch(0)
+        for h in range(2):
+            weave(nc.scalar.copy, wa_bf[h][:], wa_raw[h][:])
+        b_out(2)
+        b_out(3)
+        b_max(0)
+        b_fetch(1)
+        b_min(0)
+        for h in range(2):
+            quantize(wa_codes[:, cols(h)], wa_scales[:, cols(h)], wa_bf[h][:])
+        for t in range(PACK):
+            product(a_ps[t], xw_a, xs_a, t, wa_codes, wa_scales)
+        b_max(1)
+        b_fetch(2)
+        b_min(1)
+        for t in range(PACK):
+            a_out(t)
+        b_max(2)
+        b_fetch(3)
+        b_min(2)
+        b_max(3)
+
+        a2 = tiles("a2", [P, W], F32)
+        z_rows = tiles("z_rows", [P, PACK, HALF], BF16, 2)
+        z_bf = tiles("z_bf", [P, W], BF16)
+        z2_bf = tile("z2_bf", [P, PACK * W], BF16)
+        z2_codes = tile("z2_codes", [P, W], U32)
+        z2_scales = tile("z2_scales", [P, W], U8)
+        z_codes = tile("z_codes", [P, W], U32)
+        z_scales = tile("z_scales", [P, W], U8)
+
+        def a_fetch(t, h):
+            nc.vector.tensor_copy(a2[t][:, cols(h)], look(a_win[t], lists["n2"], h))
+
+        def a_gate(t):
+            nc.vector.tensor_tensor(s1[t][:], s1[t][:], a_win[t][:], ALU.mult)
+
+        def a_max(t, h):
+            nc.vector.tensor_tensor(a2[t][:, cols(h)], a2[t][:, cols(h)], s1[t][:, cols(h)], ALU.max)
+            nc.scalar.activation(z_rows[h][:, t, :], a2[t][:, cols(h)], ACT.Copy, scale=gt_signed[:, t : t + 1])
+
+        def z_weave(copy, h, u):
+            copy(
+                z_bf[u][:, cols(h)].rearrange("p (m t) -> p m t", t=PACK),
+                z_rows[h][:].rearrange("p t (m u) -> p u m t", u=PACK)[:, u],
+            )
+
+        a_fetch(0, 0)
+        b_min(3)
+        weave(nc.scalar.copy, z2_bf[:], z2_rows[:])
+        for t in range(PACK):
+            a_gate(t)
+            a_fetch((t + 1) % PACK, (t + 1) // PACK)
+            a_max(t, 0)
+        for u in range(PACK):
+            z_weave(nc.scalar.copy, 0, u)
+        for t in range(PACK):
+            if t + 1 < PACK:
+                a_fetch(t + 1, 1)
+            a_max(t, 1)
+        quantize(z2_codes[:], z2_scales[:], z2_bf[:])
+
+        cv_ps = [ps.tile([P, W], F32, name="cv_ps%d" % u, tag="bank%d" % u) for u in range(PACK)]
+        z_weave(nc.vector.tensor_copy, 1, 0)
+        for u in range(PACK):
+            if u + 1 < PACK:
+                z_weave(nc.vector.tensor_copy, 1, u + 1)
+            m = slice(u * P, (u + 1) * P)
+            quantize(z_codes[:, m], z_scales[:, m], z_bf[u][:])
+            product(cv_ps[u], z_codes, z_scales, u, z2_codes, z2_scales)
+
+        cv_win = tiles("cv_win", [P, W], F32)
+        sg = tiles("sg", [P, W], F32)
+        s7 = tiles("s7", [P, W], F32)
+        p5 = tiles("p5", [P, W], F32)
+        p6 = tiles("p6", [P, W], F32)
+        y = tiles("y", [P, PACK, HALF], F32, 2)
+        y_bf = tiles("y_bf", [P, PACK * HALF], BF16, 2)
+        y_codes = tile("y_codes", [P, W], U32)
+        y_scales = tile("y_scales", [P, W], U8)
+        out_rows = out_0.rearrange("(p u) n -> p u n", u=PACK)
+        out_words = out_1[0].rearrange("p n r -> p (n r)").bitcast(I32)
+        out_scales = out_2[0].bitcast(I32)
+
+        def c_gates(u, h):
+            if h == 0:
+                nc.scalar.activation(cv_win[u][:], cv_ps[u][:], ACT.Copy, scale=0.0625)
+            nc.scalar.activation(sg[u][:, cols(h)], cv_ps[u][:, cols(h)], ACT.Sigmoid, scale=0.0625)
+            nc.scalar.activation(s7[u][:, cols(h)], look(cv_win[u], lists["n7"], h), ACT.Sigmoid)
+
+        def c_fetch(u, h):
+            nc.vector.tensor_tensor(p5[u][:, cols(h)], look(cv_win[u], lists["n5"], h), sg[u][:, cols(h)], ALU.mult)
+            nc.vector.tensor_tensor(p6[u][:, cols(h)], look(cv_win[u], lists["n6"], h), s7[u][:, cols(h)], ALU.mult)
+
+        def c_sum(u, h):
+            nc.vector.tensor_tensor(y[h][:, u, :], p5[u][:, cols(h)], p6[u][:, cols(h)], ALU.add)
+            nc.sync.dma_start(out_rows[:, u, cols(h)], y[h][:, u, :])
+
+        def y_planes(h):
+            quantize(y_codes[:, cols(h)], y_scales[:, cols(h)], y_bf[h][:])
+            nc.sync.dma_start(out_words[:, cols(h)], y_codes[:, cols(h)].bitcast(I32))
+
+        steps = [(u, h) for h in range(2) for u in range(PACK)]
+        for i, (u, h) in enumerate(steps):
+            c_gates(u, h)
+            c_fetch(u, h)
+            if i > 0:
+                c_sum(*steps[i - 1])
+            if (u, h) == (1, 1):
+                weave(nc.scalar.copy, y_bf[0][:], y[0][:])
+            if (u, h) == (3, 1):
+                y_planes(0)
+        c_sum(3, 1)
+        weave(nc.vector.tensor_copy, y_bf[1][:], y[1][:])
+        y_planes(1)
+        for q in range(4):
+            eng = nc.scalar if q % 2 else nc.sync
+            eng.dma_start(out_scales[4 * q : 4 * q + 4, :], y_scales[32 * q : 32 * q + 4, :].bitcast(I32))

@@ -1,6 +1,7 @@
 from contextlib import ExitStack
 
 import concourse.mybir as mybir
+from concourse.masks import make_identity
 
 K, T, S, N, H = 512, 2048, 512, 512, 512
 FLOPS = 2 * K * S * H + 2 * K * S * N + 2 * S * H * N
@@ -28,8 +29,8 @@ def tile_picked_mombgmaxminmxwsum_none_po_kernel(tc, x_words, x_scales, wa, wb, 
         sb = ctx.enter_context(tc.tile_pool(name="sb", bufs=1))
         ps = ctx.enter_context(tc.psum_pool(name="ps", bufs=1))
 
-        def tile(name, shape, dtype):
-            return sb.tile(shape, dtype, name=name, align_bytes=64)
+        def tile(name, shape, dtype, tag=None):
+            return sb.tile(shape, dtype, name=name, tag=tag or name, align_bytes=64)
 
         def tiles(name, shape, dtype, count=PACK):
             return [tile("%s%d" % (name, i), shape, dtype) for i in range(count)]
@@ -37,8 +38,8 @@ def tile_picked_mombgmaxminmxwsum_none_po_kernel(tc, x_words, x_scales, wa, wb, 
         def cols(h):
             return slice(h * HALF, (h + 1) * HALF)
 
-        def look(window, lst, h):
-            return window[:].indirect(lst[:, h * LCOLS : (h + 1) * LCOLS])
+        def look(window, lst, c):
+            return window[:].indirect(lst[:, c.start // 16 : c.stop // 16])
 
         lists = {}
         for name in ("two", "offs", "n1", "n2", "n3", "n4", "n5", "n6", "n7"):
@@ -46,15 +47,19 @@ def tile_picked_mombgmaxminmxwsum_none_po_kernel(tc, x_words, x_scales, wa, wb, 
 
         xs = tile("xs", [P, T], U8)
         xw = tile("xw", [P, T], U32)
-        wb_raw = tiles("wb_raw", [P, PACK, HALF], F32, 2)
-        wa_raw = tiles("wa_raw", [P, PACK, HALF], F32, 2)
-        gt_sb = tile("gt_sb", [P, PACK], F32)
-        gi_sb = tile("gi_sb", [P, PACK], F32)
+        wide = tiles("wide", [P, 2 * W], F32)
+        wb_raw = [x[:].rearrange("p (j c) -> p j c", j=PACK) for x in (wide[0], wide[3])]
+        wa_raw = [x[:].rearrange("p (j c) -> p j c", j=PACK) for x in (wide[2], wide[1])]
+        wa_bf = [x[:, :W].bitcast(BF16) for x in (wide[3], wide[2])]
+        g_rows = tile("g_rows", [P, P], F32)
+        ident = tile("ident", [P, P], F32)
 
         warm = tile("warm", [P, 2], F32)
         nc.vector.memset(xs[:].bitcast(I32), 0)
         nc.gpsimd.memset(warm[:, 0:1], 0.0)
         nc.scalar.activation(warm[:, 1:2], warm[:, 0:1], ACT.Sigmoid)
+        nc.gpsimd.memset(g_rows[:], 0.0)
+        make_identity(nc, ident[:])
 
         nc.sync.dma_start(lists["two"][:], two)
         scale_rows = x_scales[0].bitcast(I32)
@@ -64,31 +69,36 @@ def tile_picked_mombgmaxminmxwsum_none_po_kernel(tc, x_words, x_scales, wa, wb, 
         wb_rows = wb.rearrange("(p j) c -> p j c", j=PACK)
         wa_rows = wa.rearrange("(p j) c -> p j c", j=PACK)
         for h in range(2):
-            nc.sync.dma_start(wb_raw[h][:], wb_rows[:, :, cols(h)])
+            nc.sync.dma_start(wb_raw[h], wb_rows[:, :, cols(h)])
+        for k, g in enumerate((gi, gt)):
+            nc.sync.dma_start(
+                g_rows[PACK * k : PACK * (k + 1), :].rearrange("t (q r) -> t q r", r=8),
+                g.rearrange("(q t r) o -> t q (r o)", t=PACK, r=8),
+            )
         nc.sync.dma_start(xw[:].bitcast(I32), x_words[0].rearrange("p n r -> p (n r)").bitcast(I32))
-        nc.sync.dma_start(gi_sb[:], gi.rearrange("(p t) o -> p (t o)", t=PACK))
-        nc.sync.dma_start(gt_sb[:], gt.rearrange("(p t) o -> p (t o)", t=PACK))
         nc.sync.dma_start(lists["n3"][:], n3)
         nc.sync.dma_start(lists["n4"][:], n4)
         for h in range(2):
-            nc.sync.dma_start(wa_raw[h][:], wa_rows[:, :, cols(h)])
+            nc.sync.dma_start(wa_raw[h], wa_rows[:, :, cols(h)])
         for name, src in (("n1", n1), ("n2", n2), ("n5", n5), ("n6", n6), ("n7", n7)):
             nc.sync.dma_start(lists[name][:], src)
 
         def pick_scales(name):
             got = tile("got_" + name, [P, S], U8)
-            dealt = tile("dealt_" + name, [P, S], U8)
             nc.vector.tensor_copy(got[:], xs[:].indirect(lists[name][:]))
-            return got, dealt
+            return got
 
-        def deal_scales(got, dealt):
+        def deal_scales(name, got, tag=None):
+            dealt = tile("dealt_" + name, [P, S], U8, tag=tag)
             nc.vector.tensor_copy(
-                dealt[:].rearrange("p (t m) -> p t m", t=PACK), got[:].rearrange("p (m t) -> p t m", t=PACK)
+                dealt[:].bitcast(I32).rearrange("p (t q w) -> p t q w", t=PACK, w=2),
+                got[:].bitcast(I32).rearrange("p (q t w) -> p t q w", t=PACK, w=2),
             )
+            return dealt
 
         def pick_words(name):
             words = tile("words_" + name, [P, S], U32)
-            nc.vector.tensor_copy(words[:].rearrange("p (t m) -> p m t", t=PACK), xw[:].indirect(lists[name][:]))
+            nc.vector.tensor_copy(words[:].rearrange("p (t q r) -> p q t r", t=PACK, r=8), xw[:].indirect(lists[name][:]))
             return words
 
         def weave(copy, dst, src):
@@ -97,60 +107,63 @@ def tile_picked_mombgmaxminmxwsum_none_po_kernel(tc, x_words, x_scales, wa, wb, 
         def quantize(codes, scales, src):
             nc.vector.quantize_mx(out=codes.bitcast(FP8X4), scales=scales, in_=src)
 
-        def product(bank, l_codes, l_scales, t, r_codes, r_scales):
+        def product(bank, l_codes, l_scales, t, r_codes, r_scales, c=slice(0, W)):
             m = slice(t * P, (t + 1) * P)
             nc.tensor.matmul_mx(
-                out=bank[:], lhsT=l_codes[:, m].bitcast(FP8X4), lhsT_scale=l_scales[:, m],
-                rhs=r_codes[:].bitcast(FP8X4), rhs_scale=r_scales[:], start=True, stop=True,
+                out=bank[:, c], lhsT=l_codes[:, m].bitcast(FP8X4), lhsT_scale=l_scales[:, m],
+                rhs=r_codes[:, c].bitcast(FP8X4), rhs_scale=r_scales[:, c], start=True, stop=True,
             )
 
-        got_b, xs_b = pick_scales("two")
-        got_a, xs_a = pick_scales("offs")
-        deal_scales(got_b, xs_b)
-        deal_scales(got_a, xs_a)
+        full = slice(0, W)
+        got_b = pick_scales("two")
+        got_a = pick_scales("offs")
+        xs_b = deal_scales("two", got_b)
 
-        wb_bf = tiles("wb_bf", [P, PACK * HALF], BF16, 2)
+        wb_bf = tile("wb_bf", [P, PACK * W], BF16)
         wb_codes = tile("wb_codes", [P, W], U32)
         wb_scales = tile("wb_scales", [P, W], U8)
         for h in range(2):
-            weave(nc.scalar.copy, wb_bf[h][:], wb_raw[h][:])
-        for h in range(2):
-            quantize(wb_codes[:, cols(h)], wb_scales[:, cols(h)], wb_bf[h][:])
+            weave(nc.scalar.copy, wb_bf[:, h * PACK * HALF : (h + 1) * PACK * HALF], wb_raw[h])
+        quantize(wb_codes[:], wb_scales[:], wb_bf[:])
         xw_b = pick_words("two")
 
+        g_ps = ps.tile([P, P], F32, name="g_ps", tag="bank7")
+        g_abs = tile("g_abs", [P, 2 * PACK], F32)
+        g_sign = tile("g_sign", [P, 2 * PACK], F32)
         sign = tile("sign", [P, PACK], F32)
-        gi_abs = tile("gi_abs", [P, PACK], F32)
-        gt_signed = tile("gt_signed", [P, PACK], F32)
-        nc.vector.tensor_scalar(sign[:], gi_sb[:], 0.0, 2.0, ALU.is_ge, ALU.mult)
-        nc.vector.scalar_tensor_tensor(gi_abs[:], gi_sb[:], -1.0, gi_sb[:], ALU.mult, ALU.max)
-        nc.vector.scalar_tensor_tensor(gt_signed[:], sign[:], 1.0, gt_sb[:], ALU.subtract, ALU.mult)
+        nc.tensor.transpose(g_ps[:], g_rows[:], ident[:])
+        nc.scalar.activation(g_abs[:], g_ps[:, : 2 * PACK], ACT.Abs)
+        nc.scalar.copy(g_sign[:], g_ps[:, : 2 * PACK])
+        nc.gpsimd.tensor_scalar(g_sign[:], g_sign[:], 0.0, 2.0, ALU.is_ge, ALU.mult)
+        nc.gpsimd.tensor_scalar(g_sign[:], g_sign[:], 1.0, -1.0, ALU.mult, ALU.add)
+        nc.gpsimd.tensor_tensor(sign[:], g_sign[:, :PACK], g_sign[:, PACK:], ALU.mult)
+        gi_abs, gt_abs = g_abs[:, :PACK], g_abs[:, PACK:]
 
         b_ps = [ps.tile([P, W], F32, name="b_ps%d" % t, tag="bank%d" % t) for t in range(PACK)]
         a_ps = [ps.tile([P, W], F32, name="a_ps%d" % t, tag="bank%d" % (PACK + t)) for t in range(PACK)]
         for t in range(PACK):
             product(b_ps[t], xw_b, xs_b, t, wb_codes, wb_scales)
+        xs_a = deal_scales("offs", got_a, tag="wb_bf")
         xw_a = pick_words("offs")
 
-        b_win = tiles("b_win", [P, W], F32)
         b_bf = tiles("b_bf", [P, W], BF16)
         b3 = tiles("b3", [P, W], BF16)
         b4 = tiles("b4", [P, W], BF16)
         z2_rows = tile("z2_rows", [P, PACK, W], BF16)
-        wa_bf = tiles("wa_bf", [P, PACK * HALF], BF16, 2)
         wa_codes = tile("wa_codes", [P, W], U32)
         wa_scales = tile("wa_scales", [P, W], U8)
         a_win = tiles("a_win", [P, W], F32)
+        ag_win = tiles("ag_win", [P, W], F32)
         s1 = tiles("s1", [P, W], F32)
 
-        def b_out(t):
-            nc.scalar.activation(b_win[t][:], b_ps[t][:], ACT.Copy, scale=gi_abs[:, t : t + 1])
-            nc.scalar.activation(b_bf[t][:], b_ps[t][:], ACT.Copy, scale=gi_abs[:, t : t + 1])
+        def b_window(t):
+            nc.scalar.activation(wide[t][:, :W], b_ps[t][:], ACT.Copy, scale=gi_abs[:, t : t + 1])
 
-        def b_fetch(t):
-            for h in range(2):
-                nc.vector.tensor_copy(b3[t][:, cols(h)], look(b_win[t], lists["n3"], h))
-            for h in range(2):
-                nc.vector.tensor_copy(b4[t][:, cols(h)], look(b_win[t], lists["n4"], h))
+        def b_round(t):
+            nc.scalar.copy(b_bf[t][:], wide[t][:, :W])
+
+        def b_fetch(dst, name, t):
+            nc.vector.tensor_copy(dst[t][:], look(wide[t], lists[name], full))
 
         def b_max(t):
             nc.vector.tensor_tensor(b3[t][:], b3[t][:], b_bf[t][:], ALU.max)
@@ -160,51 +173,54 @@ def tile_picked_mombgmaxminmxwsum_none_po_kernel(tc, x_words, x_scales, wa, wb, 
 
         def a_out(t):
             nc.scalar.copy(a_win[t][:], a_ps[t][:])
+            nc.scalar.activation(ag_win[t][:], a_ps[t][:], ACT.Copy, scale=gt_abs[:, t : t + 1])
             for h in range(2):
-                nc.scalar.activation(s1[t][:, cols(h)], look(a_win[t], lists["n1"], h), ACT.Sigmoid)
+                nc.scalar.activation(s1[t][:, cols(h)], look(a_win[t], lists["n1"], cols(h)), ACT.Sigmoid)
 
-        b_out(0)
-        b_out(1)
-        b_fetch(0)
+        def wa_weave(h):
+            weave(nc.scalar.copy, wa_bf[h], wa_raw[h])
+
+        b_window(0)
+        wa_weave(0)
+        wa_weave(1)
+        b_fetch(b3, "n3", 0)
+        b_fetch(b4, "n4", 0)
         for h in range(2):
-            weave(nc.scalar.copy, wa_bf[h][:], wa_raw[h][:])
-        b_out(2)
-        b_out(3)
+            quantize(wa_codes[:, cols(h)], wa_scales[:, cols(h)], wa_bf[h])
+        b_window(1)
+        b_round(0)
+        for k in range(PACK):
+            product(a_ps[k], xw_a, xs_a, k, wa_codes, wa_scales)
+        b_round(1)
+        for t in (2, 3):
+            b_window(t)
+            b_round(t)
+        for k in range(PACK):
+            a_out(k)
         b_max(0)
-        b_fetch(1)
-        b_min(0)
-        for h in range(2):
-            quantize(wa_codes[:, cols(h)], wa_scales[:, cols(h)], wa_bf[h][:])
-        for t in range(PACK):
-            product(a_ps[t], xw_a, xs_a, t, wa_codes, wa_scales)
-        b_max(1)
-        b_fetch(2)
-        b_min(1)
-        for t in range(PACK):
-            a_out(t)
-        b_max(2)
-        b_fetch(3)
-        b_min(2)
-        b_max(3)
+        for t in range(1, PACK):
+            b_fetch(b3, "n3", t)
+            b_min(t - 1)
+            b_fetch(b4, "n4", t)
+            b_max(t)
 
-        a2 = tiles("a2", [P, W], F32)
+        gated = tiles("gated", [P, W], BF16)
         z_rows = tiles("z_rows", [P, PACK, HALF], BF16, 2)
         z_bf = tiles("z_bf", [P, W], BF16)
         z2_bf = tile("z2_bf", [P, PACK * W], BF16)
-        z2_codes = tile("z2_codes", [P, W], U32)
         z2_scales = tile("z2_scales", [P, W], U8)
         z_codes = tile("z_codes", [P, W], U32)
         z_scales = tile("z_scales", [P, W], U8)
 
-        def a_fetch(t, h):
-            nc.vector.tensor_copy(a2[t][:, cols(h)], look(a_win[t], lists["n2"], h))
+        def a_fetch(dst, t, h):
+            nc.vector.tensor_copy(dst, look(ag_win[t], lists["n2"], cols(h)))
 
         def a_gate(t):
-            nc.vector.tensor_tensor(s1[t][:], s1[t][:], a_win[t][:], ALU.mult)
+            nc.vector.tensor_tensor(gated[t][:], s1[t][:], ag_win[t][:], ALU.mult)
 
-        def a_max(t, h):
-            nc.vector.tensor_tensor(a2[t][:, cols(h)], a2[t][:, cols(h)], s1[t][:, cols(h)], ALU.max)
-            nc.scalar.activation(z_rows[h][:, t, :], a2[t][:, cols(h)], ACT.Copy, scale=gt_signed[:, t : t + 1])
+        def a_max(dst, src, t, h):
+            nc.vector.tensor_tensor(dst, src, gated[t][:, cols(h)], ALU.max)
+            nc.scalar.activation(z_rows[h][:, t, :], dst, ACT.Copy, scale=sign[:, t : t + 1])
 
         def z_weave(copy, h, u):
             copy(
@@ -212,74 +228,103 @@ def tile_picked_mombgmaxminmxwsum_none_po_kernel(tc, x_words, x_scales, wa, wb, 
                 z_rows[h][:].rearrange("p t (m u) -> p u m t", u=PACK)[:, u],
             )
 
-        a_fetch(0, 0)
+        lo = tiles("lo", [P, HALF], BF16)
+        top = [tile("top%d" % t, [P, 2, HALF], BF16, tag="a_win%d" % ((t + 1) % PACK)) for t in range(PACK)]
+        a_fetch(lo[0][:], 0, 0)
         b_min(3)
         weave(nc.scalar.copy, z2_bf[:], z2_rows[:])
         for t in range(PACK):
             a_gate(t)
-            a_fetch((t + 1) % PACK, (t + 1) // PACK)
-            a_max(t, 0)
+            if t + 1 < PACK:
+                a_fetch(lo[t + 1][:], t + 1, 0)
+            else:
+                a_fetch(top[2][:, 1, :], 0, 1)
+            a_max(top[t][:, 0, :], lo[t][:], t, 0)
         for u in range(PACK):
             z_weave(nc.scalar.copy, 0, u)
+        hi = [top[2][:, 1, :], top[1][:, 0, :], top[2][:, 0, :], top[3][:, 0, :]]
         for t in range(PACK):
             if t + 1 < PACK:
-                a_fetch(t + 1, 1)
-            a_max(t, 1)
+                a_fetch(hi[t + 1], t + 1, 1)
+            a_max(hi[t], hi[t], t, 1)
+        z2_codes = tile("z2_codes", [P, W], U32, tag="ag_win3")
         quantize(z2_codes[:], z2_scales[:], z2_bf[:])
 
         cv_ps = [ps.tile([P, W], F32, name="cv_ps%d" % u, tag="bank%d" % u) for u in range(PACK)]
+        cv_hi = ps.tile([P, W], F32, name="cv_hi", tag="bank%d" % PACK)
         z_weave(nc.vector.tensor_copy, 1, 0)
         for u in range(PACK):
             if u + 1 < PACK:
                 z_weave(nc.vector.tensor_copy, 1, u + 1)
             m = slice(u * P, (u + 1) * P)
             quantize(z_codes[:, m], z_scales[:, m], z_bf[u][:])
-            product(cv_ps[u], z_codes, z_scales, u, z2_codes, z2_scales)
+            if u == 0:
+                product(cv_ps[0], z_codes, z_scales, 0, z2_codes, z2_scales, cols(0))
+                product(cv_hi, z_codes, z_scales, 0, z2_codes, z2_scales, cols(1))
+            else:
+                product(cv_ps[u], z_codes, z_scales, u, z2_codes, z2_scales, full)
 
-        cv_win = tiles("cv_win", [P, W], F32)
+        head, mid, tail = slice(0, 256), slice(256, 384), slice(384, W)
+        front = slice(0, 384)
         sg = tiles("sg", [P, W], F32)
         s7 = tiles("s7", [P, W], F32)
         p5 = tiles("p5", [P, W], F32)
         p6 = tiles("p6", [P, W], F32)
-        y = tiles("y", [P, PACK, HALF], F32, 2)
-        y_bf = tiles("y_bf", [P, PACK * HALF], BF16, 2)
+        y_front = tile("y_front", [P, PACK, 384], F32)
+        y_tail = tile("y_tail", [P, PACK, 128], F32)
         y_codes = tile("y_codes", [P, W], U32)
         y_scales = tile("y_scales", [P, W], U8)
         out_rows = out_0.rearrange("(p u) n -> p u n", u=PACK)
         out_words = out_1[0].rearrange("p n r -> p (n r)").bitcast(I32)
         out_scales = out_2[0].bitcast(I32)
 
-        def c_gates(u, h):
-            if h == 0:
-                nc.scalar.activation(cv_win[u][:], cv_ps[u][:], ACT.Copy, scale=0.0625)
-            nc.scalar.activation(sg[u][:, cols(h)], cv_ps[u][:, cols(h)], ACT.Sigmoid, scale=0.0625)
-            nc.scalar.activation(s7[u][:, cols(h)], look(cv_win[u], lists["n7"], h), ACT.Sigmoid)
+        def c_sigmoid(u, bank, c):
+            nc.scalar.activation(sg[u][:, c], bank[:, c], ACT.Sigmoid, scale=0.0625)
 
-        def c_fetch(u, h):
-            nc.vector.tensor_tensor(p5[u][:, cols(h)], look(cv_win[u], lists["n5"], h), sg[u][:, cols(h)], ALU.mult)
-            nc.vector.tensor_tensor(p6[u][:, cols(h)], look(cv_win[u], lists["n6"], h), s7[u][:, cols(h)], ALU.mult)
+        def c_s7(u, c):
+            nc.scalar.activation(s7[u][:, c], look(wide[u], lists["n7"], c), ACT.Sigmoid)
 
-        def c_sum(u, h):
-            nc.vector.tensor_tensor(y[h][:, u, :], p5[u][:, cols(h)], p6[u][:, cols(h)], ALU.add)
-            nc.sync.dma_start(out_rows[:, u, cols(h)], y[h][:, u, :])
+        def c_fetch(u, c):
+            nc.vector.tensor_tensor(p5[u][:, c], look(wide[u], lists["n5"], c), sg[u][:, c], ALU.mult)
+            nc.vector.tensor_tensor(p6[u][:, c], look(wide[u], lists["n6"], c), s7[u][:, c], ALU.mult)
 
-        def y_planes(h):
-            quantize(y_codes[:, cols(h)], y_scales[:, cols(h)], y_bf[h][:])
-            nc.sync.dma_start(out_words[:, cols(h)], y_codes[:, cols(h)].bitcast(I32))
+        def c_sum(y, u, c):
+            nc.vector.tensor_tensor(y[:, u, :], p5[u][:, c], p6[u][:, c], ALU.add)
+            nc.sync.dma_start(out_rows[:, u, c], y[:, u, :])
 
-        steps = [(u, h) for h in range(2) for u in range(PACK)]
-        for i, (u, h) in enumerate(steps):
-            c_gates(u, h)
-            c_fetch(u, h)
-            if i > 0:
-                c_sum(*steps[i - 1])
-            if (u, h) == (1, 1):
-                weave(nc.scalar.copy, y_bf[0][:], y[0][:])
-            if (u, h) == (3, 1):
-                y_planes(0)
-        c_sum(3, 1)
-        weave(nc.vector.tensor_copy, y_bf[1][:], y[1][:])
-        y_planes(1)
+        nc.scalar.activation(wide[0][:, cols(0)], cv_ps[0][:, cols(0)], ACT.Copy, scale=0.0625)
+        nc.vector.tensor_scalar(wide[0][:, cols(1)], cv_hi[:, cols(1)], 0.0625, None, ALU.mult)
+        c_sigmoid(0, cv_ps[0], head)
+        c_s7(0, cols(0))
+        c_sigmoid(0, cv_hi, mid)
+        c_s7(0, cols(1))
+        c_fetch(0, head)
+        c_fetch(0, mid)
+        for u in range(1, PACK):
+            nc.scalar.activation(wide[u][:, :W], cv_ps[u][:], ACT.Copy, scale=0.0625)
+            c_sigmoid(u, cv_ps[u], front)
+            c_s7(u, full)
+            c_fetch(u, front)
+            c_sum(y_front, u - 1, front)
+        for u in range(PACK):
+            c_sigmoid(u, cv_ps[u] if u else cv_hi, tail)
+        c_fetch(0, tail)
+        c_sum(y_front, 3, front)
+        bf_head = tile("bf_head", [P, PACK * 256], BF16)
+        bf_mid = tile("bf_mid", [P, PACK * 128], BF16)
+        weave(nc.scalar.copy, bf_head[:], y_front[:, :, head])
+        weave(nc.scalar.copy, bf_mid[:], y_front[:, :, mid])
+        for u in range(1, PACK):
+            c_fetch(u, tail)
+            c_sum(y_tail, u - 1, tail)
+        c_sum(y_tail, 3, tail)
+        quantize(y_codes[:, head], y_scales[:, head], bf_head[:])
+        bf_tail = tile("bf_tail", [P, PACK * 128], BF16, tag="bf_head")
+        weave(nc.vector.tensor_copy, bf_tail[:], y_tail[:])
+        quantize(y_codes[:, mid], y_scales[:, mid], bf_mid[:])
+        nc.sync.dma_start(out_words[:, front], y_codes[:, front].bitcast(I32))
+        quantize(y_codes[:, tail], y_scales[:, tail], bf_tail[:])
+        nc.scalar.dma_start(out_words[:, tail], y_codes[:, tail].bitcast(I32))
         for q in range(4):
             eng = nc.scalar if q % 2 else nc.sync
             eng.dma_start(out_scales[4 * q : 4 * q + 4, :], y_scales[32 * q : 32 * q + 4, :].bitcast(I32))

@@ -50,7 +50,7 @@ def tile_picked_mombgmaxminmxwsum_none_po_kernel(tc, x_words, x_scales, wa, wb, 
         wide = tiles("wide", [P, 2 * W], F32)
         wb_raw = [x[:].rearrange("p (j c) -> p j c", j=PACK) for x in (wide[0], wide[3])]
         wa_raw = [x[:].rearrange("p (j c) -> p j c", j=PACK) for x in (wide[2], wide[1])]
-        wa_bf = [x[:, :W].bitcast(BF16) for x in (wide[3], wide[2])]
+        wa_bf = tile("wa_bf", [P, PACK * W], BF16)
         g_rows = tile("g_rows", [P, P], F32)
         ident = tile("ident", [P, P], F32)
 
@@ -146,9 +146,6 @@ def tile_picked_mombgmaxminmxwsum_none_po_kernel(tc, x_words, x_scales, wa, wb, 
         xs_a = deal_scales("offs", got_a, tag="wb_bf")
         xw_a = pick_words("offs")
 
-        b_bf = tiles("b_bf", [P, W], BF16)
-        b3 = tiles("b3", [P, W], BF16)
-        b4 = tiles("b4", [P, W], BF16)
         z2_rows = tile("z2_rows", [P, PACK, W], BF16)
         wa_codes = tile("wa_codes", [P, W], U32)
         wa_scales = tile("wa_scales", [P, W], U8)
@@ -160,16 +157,16 @@ def tile_picked_mombgmaxminmxwsum_none_po_kernel(tc, x_words, x_scales, wa, wb, 
             nc.scalar.activation(wide[t][:, :W], b_ps[t][:], ACT.Copy, scale=gi_abs[:, t : t + 1])
 
         def b_round(t):
-            nc.scalar.copy(b_bf[t][:], wide[t][:, :W])
+            nc.scalar.copy(b_bf[t], wide[t][:, :W])
 
         def b_fetch(dst, name, t):
-            nc.vector.tensor_copy(dst[t][:], look(wide[t], lists[name], full))
+            nc.vector.tensor_copy(dst[t], look(wide[t], lists[name], full))
 
         def b_max(t):
-            nc.vector.tensor_tensor(b3[t][:], b3[t][:], b_bf[t][:], ALU.max)
+            nc.vector.tensor_tensor(b_top.get(t, b3[t]), b3[t], b_bf[t], ALU.max)
 
         def b_min(t):
-            nc.vector.tensor_tensor(z2_rows[:, t, :], b3[t][:], b4[t][:], ALU.min)
+            nc.vector.tensor_tensor(z2_rows[:, t, :], b_top.get(t, b3[t]), b4[t], ALU.min)
 
         def a_out(t):
             nc.scalar.copy(a_win[t][:], a_ps[t][:])
@@ -178,35 +175,44 @@ def tile_picked_mombgmaxminmxwsum_none_po_kernel(tc, x_words, x_scales, wa, wb, 
                 nc.scalar.activation(s1[t][:, cols(h)], look(a_win[t], lists["n1"], cols(h)), ACT.Sigmoid)
 
         def wa_weave(h):
-            weave(nc.scalar.copy, wa_bf[h], wa_raw[h])
+            nc.gpsimd.tensor_scalar(
+                wa_bf[:, h * PACK * HALF : (h + 1) * PACK * HALF].rearrange("p (c j) -> p c j", j=PACK), wa_raw[h].rearrange("p j c -> p c j"), 1.0, 0.0, ALU.mult, ALU.add
+            )
 
-        b_window(0)
+        order = (0, 3, 2, 1)
         wa_weave(0)
         wa_weave(1)
+        for t in order:
+            b_window(t)
+        first = tile("first", [P, 2, W], BF16)
+        b3, b4 = {0: first[:, 0, :]}, {0: first[:, 1, :]}
         b_fetch(b3, "n3", 0)
         b_fetch(b4, "n4", 0)
-        for h in range(2):
-            quantize(wa_codes[:, cols(h)], wa_scales[:, cols(h)], wa_bf[h])
-        b_window(1)
-        b_round(0)
+        quantize(wa_codes[:], wa_scales[:], wa_bf[:])
         for k in range(PACK):
             product(a_ps[k], xw_a, xs_a, k, wa_codes, wa_scales)
-        b_round(1)
-        for t in (2, 3):
-            b_window(t)
+        rest = tile("rest", [P, 6, W], BF16, tag="wa_bf")
+        b_bf = [x[:] for x in tiles("b_bf", [P, W], BF16)]
+        b_top = dict(b3)
+        b_top.update({0: rest[:, 5, :]})
+        last = tile("last", [P, W], BF16)
+        b3.update({t: rest[:, t - 1, :] for t in order[1:]})
+        b4.update({3: rest[:, 3, :], 2: rest[:, 4, :], 1: last[:]})
+        for t in order[1:]:
+            b_fetch(b3, "n3", t)
+            b_fetch(b4, "n4", t)
+        for t in order:
             b_round(t)
         for k in range(PACK):
             a_out(k)
-        b_max(0)
-        for t in range(1, PACK):
-            b_fetch(b3, "n3", t)
-            b_min(t - 1)
-            b_fetch(b4, "n4", t)
+        for t in order:
             b_max(t)
+        for t in order:
+            b_min(t)
 
-        gated = tiles("gated", [P, W], BF16)
+        gated = [tile("gated%d" % t, [P, W], BF16, tag="last" if t == 2 else None) for t in range(PACK)]
         z_rows = tiles("z_rows", [P, PACK, HALF], BF16, 2)
-        z_bf = tiles("z_bf", [P, W], BF16)
+        z_bf = tile("z_bf", [P, PACK, W], BF16)
         z2_bf = tile("z2_bf", [P, PACK * W], BF16)
         z2_scales = tile("z2_scales", [P, W], U8)
         z_codes = tile("z_codes", [P, W], U32)
@@ -216,7 +222,7 @@ def tile_picked_mombgmaxminmxwsum_none_po_kernel(tc, x_words, x_scales, wa, wb, 
             nc.vector.tensor_copy(dst, look(ag_win[t], lists["n2"], cols(h)))
 
         def a_gate(t):
-            nc.vector.tensor_tensor(gated[t][:], s1[t][:], ag_win[t][:], ALU.mult)
+            nc.gpsimd.tensor_tensor(gated[t][:], s1[t][:], ag_win[t][:], ALU.mult)
 
         def a_max(dst, src, t, h):
             nc.vector.tensor_tensor(dst, src, gated[t][:, cols(h)], ALU.max)
@@ -224,25 +230,25 @@ def tile_picked_mombgmaxminmxwsum_none_po_kernel(tc, x_words, x_scales, wa, wb, 
 
         def z_weave(copy, h, u):
             copy(
-                z_bf[u][:, cols(h)].rearrange("p (m t) -> p m t", t=PACK),
+                z_bf[:, u, cols(h)].rearrange("p (m t) -> p m t", t=PACK),
                 z_rows[h][:].rearrange("p t (m u) -> p u m t", u=PACK)[:, u],
             )
 
-        lo = tiles("lo", [P, HALF], BF16)
-        top = [tile("top%d" % t, [P, 2, HALF], BF16, tag="a_win%d" % ((t + 1) % PACK)) for t in range(PACK)]
-        a_fetch(lo[0][:], 0, 0)
-        b_min(3)
+        lo = tile("lo", [P, PACK, HALF], BF16)
+        top = tile("top", [P, 5, HALF], BF16, tag="a_win3")
         weave(nc.scalar.copy, z2_bf[:], z2_rows[:])
         for t in range(PACK):
             a_gate(t)
-            if t + 1 < PACK:
-                a_fetch(lo[t + 1][:], t + 1, 0)
-            else:
-                a_fetch(top[2][:, 1, :], 0, 1)
-            a_max(top[t][:, 0, :], lo[t][:], t, 0)
-        for u in range(PACK):
-            z_weave(nc.scalar.copy, 0, u)
-        hi = [top[2][:, 1, :], top[1][:, 0, :], top[2][:, 0, :], top[3][:, 0, :]]
+            a_fetch(lo[:, t, :], t, 0)
+        a_fetch(top[:, 4, :], 0, 1)
+        for t in range(PACK):
+            a_max(top[:, t, :], lo[:, t, :], t, 0)
+        nc.scalar.copy(
+            z_bf[:, :, cols(0)].rearrange("p u (c e t) -> p c u e t", e=2, t=PACK),
+            z_rows[0][:].rearrange("p t (c e u) -> p c u e t", e=2, u=PACK),
+        )
+        later = tile("later", [P, PACK, HALF], BF16, tag="lo")
+        hi = [top[:, 4, :], later[:, 1, :], later[:, 2, :], later[:, 3, :]]
         for t in range(PACK):
             if t + 1 < PACK:
                 a_fetch(hi[t + 1], t + 1, 1)
@@ -257,7 +263,7 @@ def tile_picked_mombgmaxminmxwsum_none_po_kernel(tc, x_words, x_scales, wa, wb, 
             if u + 1 < PACK:
                 z_weave(nc.vector.tensor_copy, 1, u + 1)
             m = slice(u * P, (u + 1) * P)
-            quantize(z_codes[:, m], z_scales[:, m], z_bf[u][:])
+            quantize(z_codes[:, m], z_scales[:, m], z_bf[:, u, :])
             if u == 0:
                 product(cv_ps[0], z_codes, z_scales, 0, z2_codes, z2_scales, cols(0))
                 product(cv_hi, z_codes, z_scales, 0, z2_codes, z2_scales, cols(1))

from contextlib import ExitStack

import concourse.mybir as mybir
from concourse.masks import make_identity

K, T, S, N, H = 512, 2048, 512, 512, 512
FLOPS = 2 * K * S * H + 2 * K * S * N + 2 * S * H * N

F32 = mybir.dt.float32
BF16 = mybir.dt.bfloat16
I32 = mybir.dt.int32
U32 = mybir.dt.uint32
U16 = mybir.dt.uint16
U8 = mybir.dt.uint8
FP8X4 = mybir.dt.float8_e4m3fn_x4
ALU = mybir.AluOpType
ACT = mybir.ActivationFunctionType

P = 128
PACK = 4
W = 512
HALF = 256
LCOLS = HALF // 16


def tile_picked_mombgmaxminmxwsum_none_po_kernel(tc, x_words, x_scales, wa, wb, gt, gi, offs, two, n1, n2, n3, n4, n5, n6, n7, out_0, out_1, out_2):
    nc = tc.nc
    with ExitStack() as ctx:
        sb = ctx.enter_context(tc.tile_pool(name="sb", bufs=1))
        ps = ctx.enter_context(tc.psum_pool(name="ps", bufs=1))

        def tile(name, shape, dtype, tag=None):
            return sb.tile(shape, dtype, name=name, tag=tag or name, align_bytes=64)

        def tiles(name, shape, dtype, count=PACK):
            return [tile("%s%d" % (name, i), shape, dtype) for i in range(count)]

        def cols(h):
            return slice(h * HALF, (h + 1) * HALF)

        def look(window, lst, c):
            return window[:].indirect(lst[:, c.start // 16 : c.stop // 16])

        lists = {}
        for name in ("two", "offs", "n1", "n2", "n3", "n4", "n5", "n6", "n7"):
            lists[name] = tile("list_" + name, [P, S // 16], U16)

        xs = tile("xs", [P, T], U8)
        xw = tile("xw", [P, T], U32)
        wide = tiles("wide", [P, 2 * W], F32)
        wb_raw = [x[:].rearrange("p (j c) -> p j c", j=PACK) for x in (wide[0], wide[3])]
        wa_raw = [x[:].rearrange("p (j c) -> p j c", j=PACK) for x in (wide[2], wide[1])]
        wa_bf = tile("wa_bf", [P, PACK * W], BF16)
        g_rows = tile("g_rows", [P, P], F32)
        ident = tile("ident", [P, P], F32)

        warm = tile("warm", [P, 2], F32)
        nc.vector.memset(xs[:].bitcast(I32), 0)
        nc.gpsimd.memset(warm[:, 0:1], 0.0)
        nc.scalar.activation(warm[:, 1:2], warm[:, 0:1], ACT.Sigmoid)
        nc.gpsimd.memset(g_rows[:], 0.0)
        make_identity(nc, ident[:])

        nc.sync.dma_start(lists["two"][:], two)
        scale_rows = x_scales[0].bitcast(I32)
        for q in range(4):
            nc.sync.dma_start(xs[32 * q : 32 * q + 4, :].bitcast(I32), scale_rows[4 * q : 4 * q + 4, :])
        nc.sync.dma_start(lists["offs"][:], offs)
        wb_rows = wb.rearrange("(p j) c -> p j c", j=PACK)
        wa_rows = wa.rearrange("(p j) c -> p j c", j=PACK)
        for h in range(2):
            nc.sync.dma_start(wb_raw[h], wb_rows[:, :, cols(h)])
        for k, g in enumerate((gi, gt)):
            nc.sync.dma_start(
                g_rows[PACK * k : PACK * (k + 1), :].rearrange("t (q r) -> t q r", r=8),
                g.rearrange("(q t r) o -> t q (r o)", t=PACK, r=8),
            )
        nc.sync.dma_start(xw[:].bitcast(I32), x_words[0].rearrange("p n r -> p (n r)").bitcast(I32))
        nc.sync.dma_start(lists["n3"][:], n3)
        nc.sync.dma_start(lists["n4"][:], n4)
        for h in range(2):
            nc.sync.dma_start(wa_raw[h], wa_rows[:, :, cols(h)])
        for name, src in (("n1", n1), ("n2", n2), ("n5", n5), ("n6", n6), ("n7", n7)):
            nc.sync.dma_start(lists[name][:], src)

        def pick_scales(name):
            got = tile("got_" + name, [P, S], U8)
            nc.vector.tensor_copy(got[:], xs[:].indirect(lists[name][:]))
            return got

        def deal_scales(name, got, tag=None):
            dealt = tile("dealt_" + name, [P, S], U8, tag=tag)
            nc.vector.tensor_copy(
                dealt[:].bitcast(I32).rearrange("p (t q w) -> p t q w", t=PACK, w=2),
                got[:].bitcast(I32).rearrange("p (q t w) -> p t q w", t=PACK, w=2),
            )
            return dealt

        def pick_words(name):
            words = tile("words_" + name, [P, S], U32)
            nc.vector.tensor_copy(words[:].rearrange("p (t q r) -> p q t r", t=PACK, r=8), xw[:].indirect(lists[name][:]))
            return words

        def weave(copy, dst, src):
            copy(dst.rearrange("p (c i t) -> p c t i", i=4, t=PACK), src.rearrange("p t (c i) -> p c t i", i=4))

        def quantize(codes, scales, src):
            nc.vector.quantize_mx(out=codes.bitcast(FP8X4), scales=scales, in_=src)

        def product(bank, l_codes, l_scales, t, r_codes, r_scales, c=slice(0, W)):
            m = slice(t * P, (t + 1) * P)
            nc.tensor.matmul_mx(
                out=bank[:, c], lhsT=l_codes[:, m].bitcast(FP8X4), lhsT_scale=l_scales[:, m],
                rhs=r_codes[:, c].bitcast(FP8X4), rhs_scale=r_scales[:, c], start=True, stop=True,
            )

        full = slice(0, W)
        got_b = pick_scales("two")
        got_a = pick_scales("offs")
        xs_b = deal_scales("two", got_b)

        wb_bf = tile("wb_bf", [P, PACK * W], BF16)
        wb_codes = tile("wb_codes", [P, W], U32)
        wb_scales = tile("wb_scales", [P, W], U8)
        for h in range(2):
            weave(nc.scalar.copy, wb_bf[:, h * PACK * HALF : (h + 1) * PACK * HALF], wb_raw[h])
        quantize(wb_codes[:], wb_scales[:], wb_bf[:])
        xw_b = pick_words("two")

        g_ps = ps.tile([P, P], F32, name="g_ps", tag="bank7")
        g_abs = tile("g_abs", [P, 2 * PACK], F32)
        g_sign = tile("g_sign", [P, 2 * PACK], F32)
        sign = tile("sign", [P, PACK], F32)
        nc.tensor.transpose(g_ps[:], g_rows[:], ident[:])
        nc.scalar.activation(g_abs[:], g_ps[:, : 2 * PACK], ACT.Abs)
        nc.scalar.copy(g_sign[:], g_ps[:, : 2 * PACK])
        nc.gpsimd.tensor_scalar(g_sign[:], g_sign[:], 0.0, 2.0, ALU.is_ge, ALU.mult)
        nc.gpsimd.tensor_scalar(g_sign[:], g_sign[:], 1.0, -1.0, ALU.mult, ALU.add)
        nc.gpsimd.tensor_tensor(sign[:], g_sign[:, :PACK], g_sign[:, PACK:], ALU.mult)
        gi_abs, gt_abs = g_abs[:, :PACK], g_abs[:, PACK:]

        b_ps = [ps.tile([P, W], F32, name="b_ps%d" % t, tag="bank%d" % t) for t in range(PACK)]
        a_ps = [ps.tile([P, W], F32, name="a_ps%d" % t, tag="bank%d" % (PACK + t)) for t in range(PACK)]
        for t in range(PACK):
            product(b_ps[t], xw_b, xs_b, t, wb_codes, wb_scales)
        xs_a = deal_scales("offs", got_a, tag="wb_bf")
        xw_a = pick_words("offs")

        z2_rows = tile("z2_rows", [P, PACK, W], BF16)
        wa_codes = tile("wa_codes", [P, W], U32)
        wa_scales = tile("wa_scales", [P, W], U8)
        a_win = tiles("a_win", [P, W], F32)
        ag_win = tiles("ag_win", [P, W], F32)
        s1 = tiles("s1", [P, W], F32)

        def b_window(t):
            nc.scalar.activation(wide[t][:, :W], b_ps[t][:], ACT.Copy, scale=gi_abs[:, t : t + 1])

        def b_round(t):
            nc.scalar.copy(b_bf[t], wide[t][:, :W])

        def b_fetch(dst, name, t):
            nc.vector.tensor_copy(dst[t], look(wide[t], lists[name], full))

        def b_max(t):
            nc.vector.tensor_tensor(b_top.get(t, b3[t]), b3[t], b_bf[t], ALU.max)

        def b_min(t):
            nc.vector.tensor_tensor(z2_rows[:, t, :], b_top.get(t, b3[t]), b4[t], ALU.min)

        def a_out(t):
            nc.scalar.copy(a_win[t][:], a_ps[t][:])
            nc.scalar.activation(ag_win[t][:], a_ps[t][:], ACT.Copy, scale=gt_abs[:, t : t + 1])
            for h in range(2):
                nc.scalar.activation(s1[t][:, cols(h)], look(a_win[t], lists["n1"], cols(h)), ACT.Sigmoid)

        def wa_weave(h):
            nc.gpsimd.tensor_scalar(
                wa_bf[:, h * PACK * HALF : (h + 1) * PACK * HALF].rearrange("p (c j) -> p c j", j=PACK), wa_raw[h].rearrange("p j c -> p c j"), 1.0, 0.0, ALU.mult, ALU.add
            )

        order = (0, 3, 2, 1)
        wa_weave(0)
        wa_weave(1)
        for t in order:
            b_window(t)
        first = tile("first", [P, 2, W], BF16)
        b3, b4 = {0: first[:, 0, :]}, {0: first[:, 1, :]}
        b_fetch(b3, "n3", 0)
        b_fetch(b4, "n4", 0)
        quantize(wa_codes[:], wa_scales[:], wa_bf[:])
        for k in range(PACK):
            product(a_ps[k], xw_a, xs_a, k, wa_codes, wa_scales)
        rest = tile("rest", [P, 6, W], BF16, tag="wa_bf")
        b_bf = [x[:] for x in tiles("b_bf", [P, W], BF16)]
        b_top = dict(b3)
        b_top.update({0: rest[:, 5, :]})
        last = tile("last", [P, W], BF16)
        b3.update({t: rest[:, t - 1, :] for t in order[1:]})
        b4.update({3: rest[:, 3, :], 2: rest[:, 4, :], 1: last[:]})
        for t in order[1:]:
            b_fetch(b3, "n3", t)
            b_fetch(b4, "n4", t)
        for t in order:
            b_round(t)
        for k in range(PACK):
            a_out(k)
        for t in order:
            b_max(t)
        for t in order:
            b_min(t)

        gated = [tile("gated%d" % t, [P, W], BF16, tag="last" if t == 2 else None) for t in range(PACK)]
        z_rows = tiles("z_rows", [P, PACK, HALF], BF16, 2)
        z_bf = tile("z_bf", [P, PACK, W], BF16)
        z2_bf = tile("z2_bf", [P, PACK * W], BF16)
        z2_scales = tile("z2_scales", [P, W], U8)
        z_codes = tile("z_codes", [P, W], U32)
        z_scales = tile("z_scales", [P, W], U8)

        def a_fetch(dst, t, h):
            nc.vector.tensor_copy(dst, look(ag_win[t], lists["n2"], cols(h)))

        def a_gate(t):
            nc.gpsimd.tensor_tensor(gated[t][:], s1[t][:], ag_win[t][:], ALU.mult)

        def a_max(dst, src, t, h):
            nc.vector.tensor_tensor(dst, src, gated[t][:, cols(h)], ALU.max)
            nc.scalar.activation(z_rows[h][:, t, :], dst, ACT.Copy, scale=sign[:, t : t + 1])

        def z_weave(copy, h, u):
            copy(
                z_bf[:, u, cols(h)].rearrange("p (m t) -> p m t", t=PACK),
                z_rows[h][:].rearrange("p t (m u) -> p u m t", u=PACK)[:, u],
            )

        lo = tile("lo", [P, PACK, HALF], BF16)
        top = tile("top", [P, 5, HALF], BF16, tag="a_win3")
        weave(nc.scalar.copy, z2_bf[:], z2_rows[:])
        for t in range(PACK):
            a_gate(t)
            a_fetch(lo[:, t, :], t, 0)
        a_fetch(top[:, 4, :], 0, 1)
        for t in range(PACK):
            a_max(top[:, t, :], lo[:, t, :], t, 0)
        nc.scalar.copy(
            z_bf[:, :, cols(0)].rearrange("p u (c e t) -> p c u e t", e=2, t=PACK),
            z_rows[0][:].rearrange("p t (c e u) -> p c u e t", e=2, u=PACK),
        )
        later = tile("later", [P, PACK, HALF], BF16, tag="lo")
        hi = [top[:, 4, :], later[:, 1, :], later[:, 2, :], later[:, 3, :]]
        for t in range(PACK):
            if t + 1 < PACK:
                a_fetch(hi[t + 1], t + 1, 1)
            a_max(hi[t], hi[t], t, 1)
        z2_codes = tile("z2_codes", [P, W], U32, tag="ag_win3")
        quantize(z2_codes[:], z2_scales[:], z2_bf[:])

        cv_ps = [ps.tile([P, W], F32, name="cv_ps%d" % u, tag="bank%d" % u) for u in range(PACK)]
        cv_hi = ps.tile([P, W], F32, name="cv_hi", tag="bank%d" % PACK)
        z_weave(nc.vector.tensor_copy, 1, 0)
        for u in range(PACK):
            if u + 1 < PACK:
                z_weave(nc.vector.tensor_copy, 1, u + 1)
            m = slice(u * P, (u + 1) * P)
            quantize(z_codes[:, m], z_scales[:, m], z_bf[:, u, :])
            if u == 0:
                product(cv_ps[0], z_codes, z_scales, 0, z2_codes, z2_scales, cols(0))
                product(cv_hi, z_codes, z_scales, 0, z2_codes, z2_scales, cols(1))
            else:
                product(cv_ps[u], z_codes, z_scales, u, z2_codes, z2_scales, full)

        head, mid, tail = slice(0, 256), slice(256, 384), slice(384, W)
        front = slice(0, 384)
        sg = tiles("sg", [P, W], F32)
        s7 = tiles("s7", [P, W], F32)
        p5 = tiles("p5", [P, W], F32)
        p6 = tiles("p6", [P, W], F32)
        y_front = tile("y_front", [P, PACK, 384], F32)
        y_tail = tile("y_tail", [P, PACK, 128], F32)
        y_codes = tile("y_codes", [P, W], U32)
        y_scales = tile("y_scales", [P, W], U8)
        out_rows = out_0.rearrange("(p u) n -> p u n", u=PACK)
        out_words = out_1[0].rearrange("p n r -> p (n r)").bitcast(I32)
        out_scales = out_2[0].bitcast(I32)

        def c_sigmoid(u, bank, c):
            nc.scalar.activation(sg[u][:, c], bank[:, c], ACT.Sigmoid, scale=0.0625)

        def c_s7(u, c):
            nc.scalar.activation(s7[u][:, c], look(wide[u], lists["n7"], c), ACT.Sigmoid)

        def c_fetch(u, c):
            nc.vector.tensor_tensor(p5[u][:, c], look(wide[u], lists["n5"], c), sg[u][:, c], ALU.mult)
            nc.vector.tensor_tensor(p6[u][:, c], look(wide[u], lists["n6"], c), s7[u][:, c], ALU.mult)

        def c_sum(y, u, c):
            nc.vector.tensor_tensor(y[:, u, :], p5[u][:, c], p6[u][:, c], ALU.add)
            nc.sync.dma_start(out_rows[:, u, c], y[:, u, :])

        nc.scalar.activation(wide[0][:, cols(0)], cv_ps[0][:, cols(0)], ACT.Copy, scale=0.0625)
        nc.vector.tensor_scalar(wide[0][:, cols(1)], cv_hi[:, cols(1)], 0.0625, None, ALU.mult)
        c_sigmoid(0, cv_ps[0], head)
        c_s7(0, cols(0))
        c_sigmoid(0, cv_hi, mid)
        c_s7(0, cols(1))
        c_fetch(0, head)
        c_fetch(0, mid)
        for u in range(1, PACK):
            nc.scalar.activation(wide[u][:, :W], cv_ps[u][:], ACT.Copy, scale=0.0625)
            c_sigmoid(u, cv_ps[u], front)
            c_s7(u, full)
            c_fetch(u, front)
            c_sum(y_front, u - 1, front)
        for u in range(PACK):
            c_sigmoid(u, cv_ps[u] if u else cv_hi, tail)
        c_fetch(0, tail)
        c_sum(y_front, 3, front)
        bf_head = tile("bf_head", [P, PACK * 256], BF16)
        bf_mid = tile("bf_mid", [P, PACK * 128], BF16)
        weave(nc.scalar.copy, bf_head[:], y_front[:, :, head])
        weave(nc.scalar.copy, bf_mid[:], y_front[:, :, mid])
        for u in range(1, PACK):
            c_fetch(u, tail)
            c_sum(y_tail, u - 1, tail)
        c_sum(y_tail, 3, tail)
        quantize(y_codes[:, head], y_scales[:, head], bf_head[:])
        bf_tail = tile("bf_tail", [P, PACK * 128], BF16, tag="bf_head")
        weave(nc.vector.tensor_copy, bf_tail[:], y_tail[:])
        quantize(y_codes[:, mid], y_scales[:, mid], bf_mid[:])
        nc.sync.dma_start(out_words[:, front], y_codes[:, front].bitcast(I32))
        quantize(y_codes[:, tail], y_scales[:, tail], bf_tail[:])
        nc.scalar.dma_start(out_words[:, tail], y_codes[:, tail].bitcast(I32))
        for q in range(4):
            eng = nc.scalar if q % 2 else nc.sync
            eng.dma_start(out_scales[4 * q : 4 * q + 4, :], y_scales[32 * q : 32 * q + 4, :].bitcast(I32))
